import numpy as np
import ml_dtypes


def mxq(x, axis, fmt="e4m3"):
    dtype, down = {"e4m3": (ml_dtypes.float8_e4m3fn, 7), "e5m2": (ml_dtypes.float8_e5m2, 14)}[fmt]
    v = np.moveaxis(np.asarray(x, np.float32).astype(ml_dtypes.bfloat16).astype(np.float64), axis, -1)
    blocks = v.reshape(v.shape[:-1] + (-1, 32))
    amax = np.abs(blocks).max(-1, keepdims=True)
    byte = np.maximum(np.where(amax > 0, np.frexp(amax)[1] - 1 + 127, 0) - down, 1)
    scale = np.exp2(byte - 127.0)
    codes = (blocks / scale).astype(np.float32).astype(dtype).astype(np.float64)
    return np.moveaxis((codes * scale).reshape(v.shape), -1, axis)


WIDE = False


def mx_kscale(k):
    if not WIDE:
        return np.ones(k)
    levels = np.array([24, -24, 12, -12, 0])
    if k % 512:
        return np.exp2(np.random.permutation(np.resize(levels, k // 32))).repeat(32)
    a = np.empty((k // 512, 16))
    for p in range(k // 512):
        a[p, :8] = np.random.permutation(np.resize(levels, 8))
        for g in range(8):
            far = levels[np.abs(levels - a[p, g]) >= 10]
            a[p, g + 8] = far[np.random.randint(len(far))]
    return np.exp2(a.ravel()).repeat(32)


def f64(x):
    return np.asarray(x).astype(np.float64)


def striped8(idx):
    return np.concatenate([v.reshape(-1, 16).T for v in idx]).astype(np.uint16)


def unstriped8(offs):
    return np.stack([offs[16 * g:16 * g + 16].T.reshape(-1) for g in range(8)]).astype(np.int64)


E2M1 = np.array([0.0, 0.5, 1.0, 1.5, 2.0, 3.0, 4.0, 6.0, -0.0, -0.5, -1.0, -1.5, -2.0, -3.0, -4.0, -6.0])


def pack_weight(w, fmt):
    k, n = w.shape
    w = f64(np.asarray(w, np.float32).astype(ml_dtypes.bfloat16)).reshape(k // 32, 32, n)
    amax = np.abs(w).max(1)
    if fmt == "e4m3":
        byte = np.frexp(amax)[1] - 1 + 127 - 7
    else:
        mant, ex = np.frexp(amax / 6.0)
        byte = np.where(mant > 0.5, ex, ex - 1) + 127
    byte = np.clip(np.where(amax > 0, byte, 1), 1, 254)
    scaled = (w * np.exp2(127.0 - byte)[:, None, :]).reshape(k, n).astype(np.float32)
    by_word = np.ascontiguousarray(scaled.reshape(k // 512, 128, 4, n).transpose(0, 1, 3, 2))
    if fmt == "e4m3":
        words = by_word.astype(ml_dtypes.float8_e4m3fn).view(np.uint8)
    else:
        c = by_word.astype(ml_dtypes.float4_e2m1fn).view(np.uint8) & 0xF
        words = (c[..., 0::2] | (c[..., 1::2] << 4)).reshape(k // 512, 128, 2 * n)
    return np.ascontiguousarray(words), np.ascontiguousarray(byte.astype(np.uint8).reshape(k // 512, 16, n))


def unpack_weight(words, scales, fmt):
    g, _, n = scales.shape
    words = np.ascontiguousarray(words).reshape(g, 128, n, -1)
    if fmt == "e4m3":
        vals = words.view(ml_dtypes.float8_e4m3fn).astype(np.float64)
    else:
        nib = np.empty((g, 128, n, 4), np.uint8)
        nib[..., 0::2] = words & 0xF
        nib[..., 1::2] = words >> 4
        vals = E2M1[nib]
    vals = vals * np.repeat(np.exp2(scales.astype(np.float64) - 127.0), 8, axis=1)[..., None]
    return vals.transpose(0, 1, 3, 2).reshape(g * 512, n)


K, L, N, T, J = 512, 512, 512, 2048, 1024


def setup_inputs():
    n = np.random.standard_normal
    s = mx_kscale(K)[:, None]
    s2 = mx_kscale(L)[:, None]
    p_wa = pack_weight(n((K, N)) / np.sqrt(K) / s, "e2m1")
    p_wb = pack_weight(n((L, N)) / np.sqrt(L) / s2, "e2m1")
    return {
        "xT": (n((K, T)) * s).astype(np.float32),
        "wgt": np.repeat(np.random.uniform(0.5, 2.0, (8, J)), 16, axis=0).astype(np.float32),
        "zT": (n((L, T)) * s2).astype(np.float32),
        "wgt2": np.repeat(np.random.uniform(0.5, 2.0, (8, J)), 16, axis=0).astype(np.float32),
        "wa_words": p_wa[0],
        "wa_scales": p_wa[1],
        "wb_words": p_wb[0],
        "wb_scales": p_wb[1],
        "res": (n((N, J))).astype(np.float32),
        "offs": striped8(np.stack([np.random.permutation(T)[:J] for _ in range(8)])),
        "offs2": striped8(np.stack([np.random.permutation(T)[:J] for _ in range(8)])),
    }


def reference(xT, wgt, zT, wgt2, wa_words, wa_scales, wb_words, wb_scales, res, offs, offs2):
    idx = unstriped8(offs)
    idx2 = unstriped8(offs2)
    rows = np.arange(K)
    xg = f64(wgt)[rows // 4 % 128] * f64(xT)[rows[:, None], idx[rows % 512 // 64]]
    xT_ = mxq(xg, 0, "e4m3")
    rows = np.arange(L)
    xg = f64(wgt2)[rows // 4 % 128] * f64(zT)[rows[:, None], idx2[rows % 512 // 64]]
    zT_ = mxq(xg, 0, "e4m3")
    wa_ = unpack_weight(wa_words, wa_scales, "e2m1")
    wb_ = unpack_weight(wb_words, wb_scales, "e2m1")
    ya = wa_.T @ xT_
    yb = wb_.T @ zT_
    return np.abs(ya - yb) + f64(res)

@@ -1,0 +1,180 @@
+from contextlib import ExitStack
+
+import concourse.mybir as mybir
+
+K, N, T, J = 512, 512, 2048, 1024
+FLOPS = 2 * 2 * K * N * J
+
+F32 = mybir.dt.float32
+BF16 = mybir.dt.bfloat16
+I32 = mybir.dt.int32
+U32 = mybir.dt.uint32
+U16 = mybir.dt.uint16
+U8 = mybir.dt.uint8
+FP8X4 = mybir.dt.float8_e4m3fn_x4
+FP4X4 = mybir.dt.float4_e2m1fn_x4
+ACT = mybir.ActivationFunctionType
+ALU = mybir.AluOpType
+
+P = 128
+PACK = 4
+HALF = 512
+LANES = 16
+
+
+def tile_list_absd_res_kernel(
+    tc, xT, wgt, zT, wgt2, wa_words, wa_scales, wb_words, wb_scales, res, offs, offs2, out
+):
+    nc = tc.nc
+    with ExitStack() as ctx:
+        keep = ctx.enter_context(tc.tile_pool(name="keep", bufs=1))
+        psum = ctx.enter_context(tc.psum_pool(name="psum", bufs=1))
+
+        lists = [keep.tile([P, J // LANES], U16, name="list%d" % s) for s in range(2)]
+        planes = [[keep.tile([P, T], F32, name="plane%d%d" % (s, i)) for i in range(PACK)] for s in range(2)]
+        gains = [keep.tile([P, J], F32, name="gain%d" % s) for s in range(2)]
+        picked = [keep.tile([P, PACK, J], F32, name="picked%d" % s) for s in range(2)]
+        grouped = [keep.tile([P, J, PACK], BF16, name="grouped%d" % s, align_bytes=64) for s in range(2)]
+        codes = [keep.tile([P, J], U32, name="codes%d" % s, align_bytes=64) for s in range(2)]
+        scales = [keep.tile([P, J], U8, name="scales%d" % s, align_bytes=64) for s in range(2)]
+        w_codes = [keep.tile([P, 2 * N], U8, name="w_codes%d" % s, align_bytes=64) for s in range(2)]
+        w_scales = keep.tile([P, 2, N], U8, name="w_scales", align_bytes=64)
+        resid = keep.tile([P, 2, 4, HALF], F32, name="resid")
+        absd = keep.tile([P, 2, 4, HALF], F32, name="absd")
+        result = keep.tile([P, 2, 4, HALF], F32, name="result")
+        warm = keep.tile([P, 2], F32, name="warm")
+        acc = [[psum.tile([P, HALF], F32, name="acc%d%d" % (h, m)) for m in range(4)] for h in range(2)]
+
+        src = [xT.rearrange("(p i) t -> i p t", i=PACK), zT.rearrange("(p i) t -> i p t", i=PACK)]
+        gain_src = [wgt, wgt2]
+        word_src = [wa_words, wb_words]
+        scale_src = [wa_scales, wb_scales]
+
+        def load_plane(s, i):
+            nc.sync.dma_start(planes[s][i][:], src[s][i])
+
+        def load_gain(s, a, b):
+            nc.sync.dma_start(gains[s][:, a:b], gain_src[s][:, a:b])
+
+        def load_scale(s, q):
+            nc.sync.dma_start(
+                w_scales[32 * q : 32 * q + 4, s, :].bitcast(I32),
+                scale_src[s][0, 4 * q : 4 * q + 4, :].bitcast(I32),
+            )
+
+        def load_words(s):
+            nc.sync.dma_start(w_codes[s][:].bitcast(I32), word_src[s][0].bitcast(I32))
+
+        def load_res(h, m0):
+            rows = res[m0 * P : (m0 + 2) * P, h * HALF : (h + 1) * HALF]
+            nc.sync.dma_start(resid[:, h, m0 : m0 + 2, :], rows.rearrange("(m p) j -> p m j", p=P))
+
+        def gather(s, i, a, b):
+            nc.vector.tensor_tensor(
+                picked[s][:, i, a:b],
+                planes[s][i][:].indirect(lists[s][:, a // LANES : b // LANES]),
+                gains[s][:, a:b],
+                ALU.mult,
+            )
+
+        def interleave(s, i, a, b):
+            nc.scalar.activation(
+                grouped[s][:, a:b, i : i + 2],
+                picked[s][:, i : i + 2, a:b].rearrange("p t j -> p j t"),
+                ACT.Copy,
+                scale=(1.0 if s == 0 else -1.0),
+            )
+
+        def quantize(s, a, b):
+            nc.vector.quantize_mx(
+                out=codes[s][:, a:b].bitcast(FP8X4),
+                scales=scales[s][:, a:b],
+                in_=grouped[s][:, a:b, :].rearrange("p j t -> p (j t)"),
+            )
+
+        def multiply(s, h, m):
+            cols = slice(h * HALF, (h + 1) * HALF)
+            nc.tensor.matmul_mx(
+                out=acc[h][m][:],
+                lhsT=w_codes[s][:, 2 * m * P : 2 * (m + 1) * P].bitcast(FP4X4),
+                lhsT_scale=w_scales[:, s, m * P : (m + 1) * P],
+                rhs=codes[s][:, cols].bitcast(FP8X4),
+                rhs_scale=scales[s][:, cols],
+                start=(s == 0),
+                stop=(s == 1),
+            )
+
+        def finish(h, m, a, b):
+            nc.scalar.activation(absd[:, h, m, a:b], acc[h][m][:, a:b], ACT.Abs)
+            nc.vector.tensor_tensor(result[:, h, m, a:b], absd[:, h, m, a:b], resid[:, h, m, a:b], ALU.add)
+            nc.sync.dma_start(out[m * P : (m + 1) * P, h * HALF + a : h * HALF + b], result[:, h, m, a:b])
+
+        nc.vector.memset(warm[:, 0:1], 0.0)
+        nc.scalar.activation(warm[:, 1:2], warm[:, 0:1], ACT.Abs)
+        nc.vector.memset(w_scales[:].rearrange("p s n -> p (s n)").bitcast(U32), 0)
+
+        nc.sync.dma_start(lists[0][:], offs)
+        load_plane(0, 0)
+        load_gain(0, 0, 256)
+        load_gain(0, 256, J)
+        load_plane(0, 1)
+        nc.sync.dma_start(lists[1][:], offs2)
+        load_scale(0, 0)
+        load_plane(0, 2)
+        load_scale(0, 1)
+        load_scale(0, 2)
+        load_plane(0, 3)
+        load_scale(0, 3)
+        load_gain(1, 0, HALF)
+        load_plane(1, 0)
+        load_gain(1, HALF, J)
+        load_scale(1, 0)
+        load_plane(1, 1)
+        load_scale(1, 1)
+        load_scale(1, 2)
+        load_plane(1, 2)
+        load_scale(1, 3)
+        load_words(0)
+        load_plane(1, 3)
+        load_words(1)
+        for h in range(2):
+            for m0 in (0, 2):
+                load_res(h, m0)
+
+        halves = [(0, HALF), (HALF, J)]
+        quarters = [(q * 256, (q + 1) * 256) for q in range(4)]
+
+        for a, b in [(0, 256), (256, HALF), (HALF, J)]:
+            gather(0, 0, a, b)
+        for i in (1, 2, 3):
+            for a, b in halves:
+                gather(0, i, a, b)
+                if i % 2 == 1:
+                    interleave(0, i - 1, a, b)
+        quantize(0, 0, HALF)
+        for a, b in halves:
+            gather(1, 0, a, b)
+        quantize(0, HALF, J)
+        for i in (1, 2):
+            for a, b in halves:
+                gather(1, i, a, b)
+                if i == 1:
+                    interleave(1, 0, a, b)
+        for h in range(2):
+            for m in range(4):
+                multiply(0, h, m)
+        for a, b in quarters:
+            gather(1, 3, a, b)
+            interleave(1, 2, a, b)
+        for a, b in quarters:
+            quantize(1, a, b)
+        for h in range(2):
+            for m in range(4):
+                multiply(1, h, m)
+        for h in range(2):
+            for m in range(4):
+                if (h, m) == (1, 3):
+                    finish(h, m, 0, 256)
+                    finish(h, m, 256, HALF)
+                else:
+                    finish(h, m, 0, HALF)

@@ -1,6 +1,7 @@
 from contextlib import ExitStack
 
 import concourse.mybir as mybir
+from concourse.masks import make_identity
 
 K, N, T, J = 512, 512, 2048, 1024
 FLOPS = 2 * 2 * K * N * J
@@ -31,11 +32,35 @@ def tile_list_absd_res_kernel(
         psum = ctx.enter_context(tc.psum_pool(name="psum", bufs=1))
 
         lists = [keep.tile([P, J // LANES], U16, name="list%d" % s) for s in range(2)]
-        planes = [[keep.tile([P, T], F32, name="plane%d%d" % (s, i)) for i in range(PACK)] for s in range(2)]
-        gains = [keep.tile([P, J], F32, name="gain%d" % s) for s in range(2)]
-        picked = [keep.tile([P, PACK, J], F32, name="picked%d" % s) for s in range(2)]
+        planes = [
+            [keep.tile([P, T], F32, name="plane", tag="plane%d%d" % (s, i), align_bytes=64) for i in range(PACK)]
+            for s in range(2)
+        ]
+        gain_x = keep.tile([P, J], F32, name="gain_x")
+        gain_z_head = keep.tile([P, 256], F32, name="gain_z_head", tag="gain_z_head", align_bytes=64)
+        gain_z_rest = keep.tile([P, J - 256], F32, name="gain_z_rest")
+        picked_x = keep.tile([P, PACK, J], F32, name="picked_x")
+        picked_z = keep.tile([P, 2, J], F32, name="picked_z")
+        late = {}
+        codes = {}
+
+        def gains(s, a, b):
+            if s == 0:
+                return gain_x[:, a:b]
+            if b <= 256:
+                return gain_z_head[:, a:b]
+            return gain_z_rest[:, a - 256 : b - 256]
+
+        def picked(s, i, a, b):
+            if s == 0:
+                return picked_x[:, i : i + 2, a:b]
+            if i == 0:
+                return picked_z[:, :, a:b]
+            if a not in late:
+                late[a] = keep.tile([P, 2, 256], F32, name="late", tag="late", bufs=2)
+            return late[a][:]
+
         grouped = [keep.tile([P, J, PACK], BF16, name="grouped%d" % s, align_bytes=64) for s in range(2)]
-        codes = [keep.tile([P, J], U32, name="codes%d" % s, align_bytes=64) for s in range(2)]
         scales = [keep.tile([P, J], U8, name="scales%d" % s, align_bytes=64) for s in range(2)]
         w_codes = [keep.tile([P, 2 * N], U8, name="w_codes%d" % s, align_bytes=64) for s in range(2)]
         w_scales = keep.tile([P, 2, N], U8, name="w_scales", align_bytes=64)
@@ -43,7 +68,11 @@ def tile_list_absd_res_kernel(
         absd = keep.tile([P, 2, 4, HALF], F32, name="absd")
         result = keep.tile([P, 2, 4, HALF], F32, name="result")
         warm = keep.tile([P, 2], F32, name="warm")
-        acc = [[psum.tile([P, HALF], F32, name="acc%d%d" % (h, m)) for m in range(4)] for h in range(2)]
+        ident = keep.tile([P, P], F32, name="ident")
+        gain_rows = keep.tile([P, P], F32, name="gain_rows")
+        spread = keep.tile([P, 16, 8, LANES], F32, name="spread")
+        turned = psum.tile([P, P], F32, name="turned", tag="bank0")
+        acc = {}
 
         src = [xT.rearrange("(p i) t -> i p t", i=PACK), zT.rearrange("(p i) t -> i p t", i=PACK)]
         gain_src = [wgt, wgt2]
@@ -53,11 +82,33 @@ def tile_list_absd_res_kernel(
         def load_plane(s, i):
             nc.sync.dma_start(planes[s][i][:], src[s][i])
 
-        def load_gain(s, a, b):
-            nc.sync.dma_start(gains[s][:, a:b], gain_src[s][:, a:b])
+        def load_gain(s):
+            rows = gain_src[s].rearrange("(g r) (c e) -> r g c e", r=LANES, e=P)[0]
+            nc.sync.dma_start(gain_rows[64 * s : 64 * (s + 1), :], rows)
+
+        def spread_gain(eng, s, c0, c1):
+            cols = turned[:, 64 * s : 64 * (s + 1)].rearrange("p (g c) -> p c g", c=8)[:, c0:c1, :]
+            cols = cols.unsqueeze(3).to_broadcast([P, c1 - c0, 8, LANES])
+            if eng == "vector":
+                nc.vector.tensor_copy(spread[:, 8 * s + c0 : 8 * s + c1, :, :], cols)
+            else:
+                nc.scalar.copy(spread[:, 8 * s + c0 : 8 * s + c1, :, :], cols)
+
+        def turn_gain(eng, s, c0, c1, bank):
+            back = psum.tile([P, (c1 - c0) * P], F32, name="back", tag="bank%d" % bank)
+            for c in range(c0, c1):
+                nc.tensor.transpose(
+                    back[:, (c - c0) * P : (c - c0 + 1) * P],
+                    spread[:, 8 * s + c, :, :].rearrange("p g r -> p (g r)"),
+                    ident[:],
+                )
+            if eng == "vector":
+                nc.vector.tensor_copy(gains(s, c0 * P, c1 * P), back[:])
+            else:
+                nc.scalar.copy(gains(s, c0 * P, c1 * P), back[:])
 
         def load_scale(s, q):
-            nc.sync.dma_start(
+            nc.gpsimd.dma_start(
                 w_scales[32 * q : 32 * q + 4, s, :].bitcast(I32),
                 scale_src[s][0, 4 * q : 4 * q + 4, :].bitcast(I32),
             )
@@ -71,78 +122,88 @@ def tile_list_absd_res_kernel(
 
         def gather(s, i, a, b):
             nc.vector.tensor_tensor(
-                picked[s][:, i, a:b],
+                picked(s, i - i % 2, a, b)[:, i % 2, :],
                 planes[s][i][:].indirect(lists[s][:, a // LANES : b // LANES]),
-                gains[s][:, a:b],
+                gains(s, a, b),
                 ALU.mult,
             )
 
         def interleave(s, i, a, b):
             nc.scalar.activation(
                 grouped[s][:, a:b, i : i + 2],
-                picked[s][:, i : i + 2, a:b].rearrange("p t j -> p j t"),
+                picked(s, i, a, b).rearrange("p t j -> p j t"),
                 ACT.Copy,
                 scale=(1.0 if s == 0 else -1.0),
             )
 
         def quantize(s, a, b):
+            h = a // HALF
+            if (s, h) not in codes:
+                tag = {(0, 0): "plane11", (0, 1): "gain_z_head"}.get((s, h), "codes%d" % h)
+                codes[s, h] = keep.tile([P, HALF], U32, name="codes", tag=tag, align_bytes=64)
             nc.vector.quantize_mx(
-                out=codes[s][:, a:b].bitcast(FP8X4),
+                out=codes[s, h][:, a - h * HALF : b - h * HALF].bitcast(FP8X4),
                 scales=scales[s][:, a:b],
                 in_=grouped[s][:, a:b, :].rearrange("p j t -> p (j t)"),
             )
 
         def multiply(s, h, m):
             cols = slice(h * HALF, (h + 1) * HALF)
+            if s == 0:
+                acc[h, m] = psum.tile([P, HALF], F32, name="acc", tag="bank%d" % (4 * h + m))
             nc.tensor.matmul_mx(
-                out=acc[h][m][:],
+                out=acc[h, m][:],
                 lhsT=w_codes[s][:, 2 * m * P : 2 * (m + 1) * P].bitcast(FP4X4),
                 lhsT_scale=w_scales[:, s, m * P : (m + 1) * P],
-                rhs=codes[s][:, cols].bitcast(FP8X4),
+                rhs=codes[s, h][:].bitcast(FP8X4),
                 rhs_scale=scales[s][:, cols],
                 start=(s == 0),
                 stop=(s == 1),
             )
 
         def finish(h, m, a, b):
-            nc.scalar.activation(absd[:, h, m, a:b], acc[h][m][:, a:b], ACT.Abs)
+            nc.scalar.activation(absd[:, h, m, a:b], acc[h, m][:, a:b], ACT.Abs)
             nc.vector.tensor_tensor(result[:, h, m, a:b], absd[:, h, m, a:b], resid[:, h, m, a:b], ALU.add)
             nc.sync.dma_start(out[m * P : (m + 1) * P, h * HALF + a : h * HALF + b], result[:, h, m, a:b])
 
+        load_gain(0)
+        load_gain(1)
+        make_identity(nc, ident[:])
         nc.vector.memset(warm[:, 0:1], 0.0)
         nc.scalar.activation(warm[:, 1:2], warm[:, 0:1], ACT.Abs)
-        nc.vector.memset(w_scales[:].rearrange("p s n -> p (s n)").bitcast(U32), 0)
+        nc.gpsimd.memset(w_scales[:].rearrange("p s n -> p (s n)").bitcast(U32), 0)
+        for s in range(2):
+            for q in range(4):
+                load_scale(s, q)
 
-        nc.sync.dma_start(lists[0][:], offs)
         load_plane(0, 0)
-        load_gain(0, 0, 256)
-        load_gain(0, 256, J)
-        load_plane(0, 1)
+        nc.sync.dma_start(gain_x[:, 0:256], wgt[:, 0:256])
+        nc.sync.dma_start(lists[0][:], offs)
+        for i in range(1, PACK):
+            load_plane(0, i)
         nc.sync.dma_start(lists[1][:], offs2)
-        load_scale(0, 0)
-        load_plane(0, 2)
-        load_scale(0, 1)
-        load_scale(0, 2)
-        load_plane(0, 3)
-        load_scale(0, 3)
-        load_gain(1, 0, HALF)
         load_plane(1, 0)
-        load_gain(1, HALF, J)
-        load_scale(1, 0)
-        load_plane(1, 1)
-        load_scale(1, 1)
-        load_scale(1, 2)
-        load_plane(1, 2)
-        load_scale(1, 3)
         load_words(0)
-        load_plane(1, 3)
+        load_plane(1, 1)
         load_words(1)
+        load_plane(1, 2)
+        load_plane(1, 3)
         for h in range(2):
             for m0 in (0, 2):
                 load_res(h, m0)
 
         halves = [(0, HALF), (HALF, J)]
         quarters = [(q * 256, (q + 1) * 256) for q in range(4)]
+
+        nc.tensor.transpose(turned[:], gain_rows[:], ident[:])
+        spread_gain("scalar", 0, 2, 4)
+        spread_gain("scalar", 0, 4, 8)
+        turn_gain("scalar", 0, 2, 4, 2)
+        turn_gain("scalar", 0, 4, 8, 3)
+        spread_gain("scalar", 1, 0, 8)
+        turn_gain("scalar", 1, 0, 2, 4)
+        turn_gain("scalar", 1, 2, 6, 5)
+        turn_gain("scalar", 1, 6, 8, 6)
 
         for a, b in [(0, 256), (256, HALF), (HALF, J)]:
             gather(0, 0, a, b)
@@ -151,23 +212,31 @@ def tile_list_absd_res_kernel(
                 gather(0, i, a, b)
                 if i % 2 == 1:
                     interleave(0, i - 1, a, b)
-        quantize(0, 0, HALF)
-        for a, b in halves:
-            gather(1, 0, a, b)
-        quantize(0, HALF, J)
-        for i in (1, 2):
-            for a, b in halves:
+        for i in (0, 1):
+            for a, b in [(0, 256), (256, J)]:
                 gather(1, i, a, b)
                 if i == 1:
                     interleave(1, 0, a, b)
-        for h in range(2):
-            for m in range(4):
-                multiply(0, h, m)
-        for a, b in quarters:
+        quantize(0, 0, HALF)
+        for m in range(4):
+            multiply(0, 0, m)
+        for a, b in quarters[:2]:
+            gather(1, 2, a, b)
+        for a, b in quarters[:2]:
             gather(1, 3, a, b)
             interleave(1, 2, a, b)
-        for a, b in quarters:
-            quantize(1, a, b)
+        quantize(0, HALF, J)
+        for m in range(4):
+            multiply(0, 1, m)
+        gather(1, 2, *quarters[2])
+        gather(1, 3, *quarters[2])
+        interleave(1, 2, *quarters[2])
+        quantize(1, 0, HALF)
+        gather(1, 2, *quarters[3])
+        gather(1, 3, *quarters[3])
+        interleave(1, 2, *quarters[3])
+        quantize(1, *quarters[2])
+        quantize(1, *quarters[3])
         for h in range(2):
             for m in range(4):
                 multiply(1, h, m)

@@ -70,7 +70,7 @@ def tile_list_absd_res_kernel(
         warm = keep.tile([P, 2], F32, name="warm")
         ident = keep.tile([P, P], F32, name="ident")
         gain_rows = keep.tile([P, P], F32, name="gain_rows")
-        spread = keep.tile([P, 16, 8, LANES], F32, name="spread")
+        spread = {}
         turned = psum.tile([P, P], F32, name="turned", tag="bank0")
         acc = {}
 
@@ -89,17 +89,16 @@ def tile_list_absd_res_kernel(
         def spread_gain(eng, s, c0, c1):
             cols = turned[:, 64 * s : 64 * (s + 1)].rearrange("p (g c) -> p c g", c=8)[:, c0:c1, :]
             cols = cols.unsqueeze(3).to_broadcast([P, c1 - c0, 8, LANES])
-            if eng == "vector":
-                nc.vector.tensor_copy(spread[:, 8 * s + c0 : 8 * s + c1, :, :], cols)
-            else:
-                nc.scalar.copy(spread[:, 8 * s + c0 : 8 * s + c1, :, :], cols)
+            if s not in spread:
+                spread[s] = keep.tile([P, 8, 8, LANES], F32, name="spread", tag="spread")
+            nc.scalar.copy(spread[s][:, c0:c1, :, :], cols)
 
         def turn_gain(eng, s, c0, c1, bank):
             back = psum.tile([P, (c1 - c0) * P], F32, name="back", tag="bank%d" % bank)
             for c in range(c0, c1):
                 nc.tensor.transpose(
                     back[:, (c - c0) * P : (c - c0 + 1) * P],
-                    spread[:, 8 * s + c, :, :].rearrange("p g r -> p (g r)"),
+                    spread[s][:, c, :, :].rearrange("p g r -> p (g r)"),
                     ident[:],
                 )
             if eng == "vector":
@@ -108,7 +107,7 @@ def tile_list_absd_res_kernel(
                 nc.scalar.copy(gains(s, c0 * P, c1 * P), back[:])
 
         def load_scale(s, q):
-            nc.gpsimd.dma_start(
+            nc.sync.dma_start(
                 w_scales[32 * q : 32 * q + 4, s, :].bitcast(I32),
                 scale_src[s][0, 4 * q : 4 * q + 4, :].bitcast(I32),
             )
@@ -172,22 +171,28 @@ def tile_list_absd_res_kernel(
         nc.vector.memset(warm[:, 0:1], 0.0)
         nc.scalar.activation(warm[:, 1:2], warm[:, 0:1], ACT.Abs)
         nc.gpsimd.memset(w_scales[:].rearrange("p s n -> p (s n)").bitcast(U32), 0)
-        for s in range(2):
-            for q in range(4):
-                load_scale(s, q)
 
         load_plane(0, 0)
         nc.sync.dma_start(gain_x[:, 0:256], wgt[:, 0:256])
         nc.sync.dma_start(lists[0][:], offs)
-        for i in range(1, PACK):
-            load_plane(0, i)
+        load_plane(0, 1)
+        load_plane(0, 2)
+        load_scale(0, 0)
+        load_plane(0, 3)
+        load_scale(0, 1)
         nc.sync.dma_start(lists[1][:], offs2)
         load_plane(1, 0)
-        load_words(0)
+        load_scale(0, 2)
+        load_scale(0, 3)
         load_plane(1, 1)
-        load_words(1)
+        load_words(0)
+        load_scale(1, 0)
         load_plane(1, 2)
+        load_scale(1, 1)
+        load_scale(1, 2)
         load_plane(1, 3)
+        load_scale(1, 3)
+        load_words(1)
         for h in range(2):
             for m0 in (0, 2):
                 load_res(h, m0)
@@ -208,15 +213,15 @@ def tile_list_absd_res_kernel(
         for a, b in [(0, 256), (256, HALF), (HALF, J)]:
             gather(0, 0, a, b)
         for i in (1, 2, 3):
-            for a, b in halves:
+            for a, b in [(0, 640), (640, J)]:
                 gather(0, i, a, b)
                 if i % 2 == 1:
                     interleave(0, i - 1, a, b)
-        for i in (0, 1):
-            for a, b in [(0, 256), (256, J)]:
-                gather(1, i, a, b)
-                if i == 1:
-                    interleave(1, 0, a, b)
+        for a, b in [(0, 256), (256, J)]:
+            gather(1, 0, a, b)
+        for a, b in [(0, 256), (256, 640), (640, J)]:
+            gather(1, 1, a, b)
+            interleave(1, 0, a, b)
         quantize(0, 0, HALF)
         for m in range(4):
             multiply(0, 0, m)

from contextlib import ExitStack

import concourse.mybir as mybir
from concourse.masks import make_identity

K, N, T, J = 512, 512, 2048, 1024
FLOPS = 2 * 2 * K * N * J

F32 = mybir.dt.float32
BF16 = mybir.dt.bfloat16
I32 = mybir.dt.int32
U32 = mybir.dt.uint32
U16 = mybir.dt.uint16
U8 = mybir.dt.uint8
FP8X4 = mybir.dt.float8_e4m3fn_x4
FP4X4 = mybir.dt.float4_e2m1fn_x4
ACT = mybir.ActivationFunctionType
ALU = mybir.AluOpType

P = 128
PACK = 4
HALF = 512
LANES = 16


def tile_list_absd_res_kernel(
    tc, xT, wgt, zT, wgt2, wa_words, wa_scales, wb_words, wb_scales, res, offs, offs2, out
):
    nc = tc.nc
    with ExitStack() as ctx:
        keep = ctx.enter_context(tc.tile_pool(name="keep", bufs=1))
        psum = ctx.enter_context(tc.psum_pool(name="psum", bufs=1))

        lists = [keep.tile([P, J // LANES], U16, name="list%d" % s) for s in range(2)]
        planes = [
            [keep.tile([P, T], F32, name="plane", tag="plane%d%d" % (s, i), align_bytes=64) for i in range(PACK)]
            for s in range(2)
        ]
        gain_x = keep.tile([P, J], F32, name="gain_x")
        gain_z_head = keep.tile([P, 256], F32, name="gain_z_head", tag="gain_z_head", align_bytes=64)
        gain_z_rest = keep.tile([P, J - 256], F32, name="gain_z_rest")
        picked_x = keep.tile([P, PACK, J], F32, name="picked_x")
        picked_z = keep.tile([P, 2, J], F32, name="picked_z")
        late = {}
        codes = {}

        def gains(s, a, b):
            if s == 0:
                return gain_x[:, a:b]
            if b <= 256:
                return gain_z_head[:, a:b]
            return gain_z_rest[:, a - 256 : b - 256]

        def picked(s, i, a, b):
            if s == 0:
                return picked_x[:, i : i + 2, a:b]
            if i == 0:
                return picked_z[:, :, a:b]
            if a not in late:
                late[a] = keep.tile([P, 2, 256], F32, name="late", tag="late", bufs=2)
            return late[a][:]

        grouped = [keep.tile([P, J, PACK], BF16, name="grouped%d" % s, align_bytes=64) for s in range(2)]
        scales = [keep.tile([P, J], U8, name="scales%d" % s, align_bytes=64) for s in range(2)]
        w_codes = [keep.tile([P, 2 * N], U8, name="w_codes%d" % s, align_bytes=64) for s in range(2)]
        w_scales = keep.tile([P, 2, N], U8, name="w_scales", align_bytes=64)
        resid = keep.tile([P, 2, 4, HALF], F32, name="resid")
        absd = keep.tile([P, 2, 4, HALF], F32, name="absd")
        result = keep.tile([P, 2, 4, HALF], F32, name="result")
        warm = keep.tile([P, 2], F32, name="warm")
        ident = keep.tile([P, P], F32, name="ident")
        gain_rows = keep.tile([P, P], F32, name="gain_rows")
        spread = {}
        turned = psum.tile([P, P], F32, name="turned", tag="bank0")
        acc = {}

        src = [xT.rearrange("(p i) t -> i p t", i=PACK), zT.rearrange("(p i) t -> i p t", i=PACK)]
        gain_src = [wgt, wgt2]
        word_src = [wa_words, wb_words]
        scale_src = [wa_scales, wb_scales]

        def load_plane(s, i):
            nc.sync.dma_start(planes[s][i][:], src[s][i])

        def load_gain(s):
            rows = gain_src[s].rearrange("(g r) (c e) -> r g c e", r=LANES, e=P)[0]
            nc.sync.dma_start(gain_rows[64 * s : 64 * (s + 1), :], rows)

        def spread_gain(eng, s, c0, c1):
            cols = turned[:, 64 * s : 64 * (s + 1)].rearrange("p (g c) -> p c g", c=8)[:, c0:c1, :]
            cols = cols.unsqueeze(3).to_broadcast([P, c1 - c0, 8, LANES])
            if s not in spread:
                spread[s] = keep.tile([P, 8, 8, LANES], F32, name="spread", tag="spread")
            nc.scalar.copy(spread[s][:, c0:c1, :, :], cols)

        def turn_gain(eng, s, c0, c1, bank):
            back = psum.tile([P, (c1 - c0) * P], F32, name="back", tag="bank%d" % bank)
            for c in range(c0, c1):
                nc.tensor.transpose(
                    back[:, (c - c0) * P : (c - c0 + 1) * P],
                    spread[s][:, c, :, :].rearrange("p g r -> p (g r)"),
                    ident[:],
                )
            if eng == "vector":
                nc.vector.tensor_copy(gains(s, c0 * P, c1 * P), back[:])
            else:
                nc.scalar.copy(gains(s, c0 * P, c1 * P), back[:])

        def load_scale(s, q):
            nc.sync.dma_start(
                w_scales[32 * q : 32 * q + 4, s, :].bitcast(I32),
                scale_src[s][0, 4 * q : 4 * q + 4, :].bitcast(I32),
            )

        def load_words(s):
            nc.sync.dma_start(w_codes[s][:].bitcast(I32), word_src[s][0].bitcast(I32))

        def load_res(h, m0):
            rows = res[m0 * P : (m0 + 2) * P, h * HALF : (h + 1) * HALF]
            nc.sync.dma_start(resid[:, h, m0 : m0 + 2, :], rows.rearrange("(m p) j -> p m j", p=P))

        def gather(s, i, a, b):
            nc.vector.tensor_tensor(
                picked(s, i - i % 2, a, b)[:, i % 2, :],
                planes[s][i][:].indirect(lists[s][:, a // LANES : b // LANES]),
                gains(s, a, b),
                ALU.mult,
            )

        def interleave(s, i, a, b):
            nc.scalar.activation(
                grouped[s][:, a:b, i : i + 2],
                picked(s, i, a, b).rearrange("p t j -> p j t"),
                ACT.Copy,
                scale=(1.0 if s == 0 else -1.0),
            )

        def quantize(s, a, b):
            h = a // HALF
            if (s, h) not in codes:
                tag = {(0, 0): "plane11", (0, 1): "gain_z_head"}.get((s, h), "codes%d" % h)
                codes[s, h] = keep.tile([P, HALF], U32, name="codes", tag=tag, align_bytes=64)
            nc.vector.quantize_mx(
                out=codes[s, h][:, a - h * HALF : b - h * HALF].bitcast(FP8X4),
                scales=scales[s][:, a:b],
                in_=grouped[s][:, a:b, :].rearrange("p j t -> p (j t)"),
            )

        def multiply(s, h, m):
            cols = slice(h * HALF, (h + 1) * HALF)
            if s == 0:
                acc[h, m] = psum.tile([P, HALF], F32, name="acc", tag="bank%d" % (4 * h + m))
            nc.tensor.matmul_mx(
                out=acc[h, m][:],
                lhsT=w_codes[s][:, 2 * m * P : 2 * (m + 1) * P].bitcast(FP4X4),
                lhsT_scale=w_scales[:, s, m * P : (m + 1) * P],
                rhs=codes[s, h][:].bitcast(FP8X4),
                rhs_scale=scales[s][:, cols],
                start=(s == 0),
                stop=(s == 1),
            )

        def finish(h, m, a, b):
            nc.scalar.activation(absd[:, h, m, a:b], acc[h, m][:, a:b], ACT.Abs)
            nc.vector.tensor_tensor(result[:, h, m, a:b], absd[:, h, m, a:b], resid[:, h, m, a:b], ALU.add)
            nc.sync.dma_start(out[m * P : (m + 1) * P, h * HALF + a : h * HALF + b], result[:, h, m, a:b])

        load_gain(0)
        load_gain(1)
        make_identity(nc, ident[:])
        nc.vector.memset(warm[:, 0:1], 0.0)
        nc.scalar.activation(warm[:, 1:2], warm[:, 0:1], ACT.Abs)
        nc.gpsimd.memset(w_scales[:].rearrange("p s n -> p (s n)").bitcast(U32), 0)

        load_plane(0, 0)
        nc.sync.dma_start(gain_x[:, 0:256], wgt[:, 0:256])
        nc.sync.dma_start(lists[0][:], offs)
        load_plane(0, 1)
        load_plane(0, 2)
        load_scale(0, 0)
        load_plane(0, 3)
        load_scale(0, 1)
        nc.sync.dma_start(lists[1][:], offs2)
        load_plane(1, 0)
        load_scale(0, 2)
        load_scale(0, 3)
        load_plane(1, 1)
        load_words(0)
        load_scale(1, 0)
        load_plane(1, 2)
        load_scale(1, 1)
        load_scale(1, 2)
        load_plane(1, 3)
        load_scale(1, 3)
        load_words(1)
        for h in range(2):
            for m0 in (0, 2):
                load_res(h, m0)

        halves = [(0, HALF), (HALF, J)]
        quarters = [(q * 256, (q + 1) * 256) for q in range(4)]

        nc.tensor.transpose(turned[:], gain_rows[:], ident[:])
        spread_gain("scalar", 0, 2, 4)
        spread_gain("scalar", 0, 4, 8)
        turn_gain("scalar", 0, 2, 4, 2)
        turn_gain("scalar", 0, 4, 8, 3)
        spread_gain("scalar", 1, 0, 8)
        turn_gain("scalar", 1, 0, 2, 4)
        turn_gain("scalar", 1, 2, 6, 5)
        turn_gain("scalar", 1, 6, 8, 6)

        for a, b in [(0, 256), (256, HALF), (HALF, J)]:
            gather(0, 0, a, b)
        for i in (1, 2, 3):
            for a, b in [(0, 640), (640, J)]:
                gather(0, i, a, b)
                if i % 2 == 1:
                    interleave(0, i - 1, a, b)
        for a, b in [(0, 256), (256, J)]:
            gather(1, 0, a, b)
        for a, b in [(0, 256), (256, 640), (640, J)]:
            gather(1, 1, a, b)
            interleave(1, 0, a, b)
        quantize(0, 0, HALF)
        for m in range(4):
            multiply(0, 0, m)
        for a, b in quarters[:2]:
            gather(1, 2, a, b)
        for a, b in quarters[:2]:
            gather(1, 3, a, b)
            interleave(1, 2, a, b)
        quantize(0, HALF, J)
        for m in range(4):
            multiply(0, 1, m)
        gather(1, 2, *quarters[2])
        gather(1, 3, *quarters[2])
        interleave(1, 2, *quarters[2])
        quantize(1, 0, HALF)
        gather(1, 2, *quarters[3])
        gather(1, 3, *quarters[3])
        interleave(1, 2, *quarters[3])
        quantize(1, *quarters[2])
        quantize(1, *quarters[3])
        for h in range(2):
            for m in range(4):
                multiply(1, h, m)
        for h in range(2):
            for m in range(4):
                if (h, m) == (1, 3):
                    finish(h, m, 0, 256)
                    finish(h, m, 256, HALF)
                else:
                    finish(h, m, 0, HALF)
